import numpy as np
import ml_dtypes


def mxq(x, axis, fmt="e4m3"):
    dtype, down = {"e4m3": (ml_dtypes.float8_e4m3fn, 7), "e5m2": (ml_dtypes.float8_e5m2, 14)}[fmt]
    v = np.moveaxis(np.asarray(x, np.float32).astype(ml_dtypes.bfloat16).astype(np.float64), axis, -1)
    blocks = v.reshape(v.shape[:-1] + (-1, 32))
    amax = np.abs(blocks).max(-1, keepdims=True)
    byte = np.maximum(np.where(amax > 0, np.frexp(amax)[1] - 1 + 127, 0) - down, 1)
    scale = np.exp2(byte - 127.0)
    codes = (blocks / scale).astype(np.float32).astype(dtype).astype(np.float64)
    return np.moveaxis((codes * scale).reshape(v.shape), -1, axis)


WIDE = False


def mx_kscale(k):
    if not WIDE:
        return np.ones(k)
    levels = np.array([10, -10, 5, -5, 0])
    if k % 512:
        return np.exp2(np.random.permutation(np.resize(levels, k // 32))).repeat(32)
    a = np.empty((k // 512, 16))
    for p in range(k // 512):
        a[p, :8] = np.random.permutation(np.resize(levels, 8))
        for g in range(8):
            far = levels[np.abs(levels - a[p, g]) >= 10]
            a[p, g + 8] = far[np.random.randint(len(far))]
    return np.exp2(a.ravel()).repeat(32)


def f64(x):
    return np.asarray(x).astype(np.float64)


def striped8(idx):
    return np.concatenate([v.reshape(-1, 16).T for v in idx]).astype(np.uint16)


def unstriped8(offs):
    return np.stack([offs[16 * g:16 * g + 16].T.reshape(-1) for g in range(8)]).astype(np.int64)


E2M1 = np.array([0.0, 0.5, 1.0, 1.5, 2.0, 3.0, 4.0, 6.0, -0.0, -0.5, -1.0, -1.5, -2.0, -3.0, -4.0, -6.0])


def pack_weight(w, fmt):
    k, n = w.shape
    w = f64(np.asarray(w, np.float32).astype(ml_dtypes.bfloat16)).reshape(k // 32, 32, n)
    amax = np.abs(w).max(1)
    if fmt == "e4m3":
        byte = np.frexp(amax)[1] - 1 + 127 - 7
    else:
        mant, ex = np.frexp(amax / 6.0)
        byte = np.where(mant > 0.5, ex, ex - 1) + 127
    byte = np.clip(np.where(amax > 0, byte, 1), 1, 254)
    scaled = (w * np.exp2(127.0 - byte)[:, None, :]).reshape(k, n).astype(np.float32)
    by_word = np.ascontiguousarray(scaled.reshape(k // 512, 128, 4, n).transpose(0, 1, 3, 2))
    if fmt == "e4m3":
        words = by_word.astype(ml_dtypes.float8_e4m3fn).view(np.uint8)
    else:
        c = by_word.astype(ml_dtypes.float4_e2m1fn).view(np.uint8) & 0xF
        words = (c[..., 0::2] | (c[..., 1::2] << 4)).reshape(k // 512, 128, 2 * n)
    return np.ascontiguousarray(words), np.ascontiguousarray(byte.astype(np.uint8).reshape(k // 512, 16, n))


def unpack_weight(words, scales, fmt):
    g, _, n = scales.shape
    words = np.ascontiguousarray(words).reshape(g, 128, n, -1)
    if fmt == "e4m3":
        vals = words.view(ml_dtypes.float8_e4m3fn).astype(np.float64)
    else:
        nib = np.empty((g, 128, n, 4), np.uint8)
        nib[..., 0::2] = words & 0xF
        nib[..., 1::2] = words >> 4
        vals = E2M1[nib]
    vals = vals * np.repeat(np.exp2(scales.astype(np.float64) - 127.0), 8, axis=1)[..., None]
    return vals.transpose(0, 1, 3, 2).reshape(g * 512, n)


def silu(v):
    return v / (1.0 + np.exp(-np.maximum(v, -700.0)))


K, M, T, S = 1024, 1024, 1024, 512


def setup_inputs():
    n = np.random.standard_normal
    s = mx_kscale(K)[:, None]
    p_w = pack_weight(n((K, M)) / np.sqrt(K) / s, "e4m3")
    return {
        "xT": (n((K, T)) * s).astype(np.float32),
        "w_words": p_w[0],
        "w_scales": p_w[1],
        "wgt": np.repeat(np.random.uniform(0.5, 2.0, (8, S)), 16, axis=0).astype(np.float32),
        "b": (0.3 * n(1024)).astype(np.float32),
        "wgo": np.repeat(np.random.uniform(0.5, 2.0, (8, S)), 16, axis=0).astype(np.float32),
        "offs": striped8(np.stack([np.random.permutation(T)[:S] for _ in range(8)])),
        "offs2": striped8(np.stack([np.random.permutation(T)[:S] for _ in range(8)])),
    }


def reference(xT, w_words, w_scales, wgt, b, wgo, offs, offs2):
    idx = unstriped8(offs)
    group = np.arange(K) % 512 // 64
    xg = f64(wgt)[np.arange(K) // 4 % 128] * f64(xT)[np.arange(K)[:, None], idx[group]]
    xT_ = mxq(xg, 0, "e4m3")
    w_ = unpack_weight(w_words, w_scales, "e4m3")
    y = w_.T @ xT_
    place = unstriped8(offs2)[np.arange(M) % 128 // 16]
    out = np.zeros((M, T))
    out[np.arange(M)[:, None], place] = f64(wgo)[np.arange(M) % 128] * (silu(y + f64(b)[:, None]))
    return out

@@ -1,0 +1,161 @@
+from contextlib import ExitStack
+
+import concourse.mybir as mybir
+from concourse.masks import make_identity
+
+K, M, T, S = 1024, 1024, 1024, 512
+FLOPS = 2 * K * M * S
+
+P = 128
+PACK = 4
+PASSES = K // (P * PACK)
+ROW_TILES = M // P
+HALVES = 2
+SH = S // HALVES
+OH = SH // 16
+
+F32 = mybir.dt.float32
+BF16 = mybir.dt.bfloat16
+I32 = mybir.dt.int32
+U32 = mybir.dt.uint32
+U16 = mybir.dt.uint16
+U8 = mybir.dt.uint8
+FP8X4 = mybir.dt.float8_e4m3fn_x4
+MULT = mybir.AluOpType.mult
+SILU = mybir.ActivationFunctionType.Silu
+
+
+def tile_list_hboth_silu_kernel(tc, xT, w_words, w_scales, wgt, b, wgo, offs, offs2, out):
+    nc = tc.nc
+    with ExitStack() as ctx:
+        keep = ctx.enter_context(tc.tile_pool(name="keep", bufs=1))
+        ypool = ctx.enter_context(tc.tile_pool(name="ypool", bufs=16))
+        psum = ctx.enter_context(tc.psum_pool(name="psum", bufs=8))
+
+        offs_sb = keep.tile([P, S // 16], U16, name="offs_sb")
+        offs2_sb = keep.tile([P, S // 16], U16, name="offs2_sb")
+        wgt_sb = [keep.tile([P, SH], F32, name=f"wgt{h}") for h in range(HALVES)]
+        wgo_sb = [keep.tile([P, SH], F32, name=f"wgo{h}") for h in range(HALVES)]
+        x_sb = [[keep.tile([P, T], F32, name=f"x{a}_{i}") for i in range(PACK)] for a in range(PASSES)]
+        g_sb = [[keep.tile([P, PACK, SH], F32, name=f"g{a}_{h}") for h in range(HALVES)] for a in range(PASSES)]
+        xb_sb = [[keep.tile([P, SH, PACK], BF16, name=f"xb{a}_{h}", align_bytes=64) for h in range(HALVES)] for a in range(PASSES)]
+        xq_sb = [[keep.tile([P, SH], U32, name=f"xq{a}_{h}", align_bytes=64) for h in range(HALVES)] for a in range(PASSES)]
+        xs_sb = [[keep.tile([P, SH], U8, name=f"xs{a}_{h}", align_bytes=64) for h in range(HALVES)] for a in range(PASSES)]
+        w_sb = [keep.tile([P, PASSES, M // 2], I32, name=f"w{c}", align_bytes=64) for c in range(2)]
+        ws_sb = keep.tile([P, M], U8, name="ws_sb", align_bytes=64)
+        win_sb = [keep.tile([P, T], F32, name=f"win{r}") for r in range(ROW_TILES)]
+        brow = keep.tile([P, P], F32, name="brow")
+        ident = keep.tile([P, P], F32, name="ident")
+        bcol = keep.tile([P, ROW_TILES], F32, name="bcol")
+        warm = keep.tile([P, 1], F32, name="warm")
+
+        x_view = xT.rearrange("(a p i) t -> a i p t", p=P, i=PACK)
+        w_view = w_words.rearrange("a p n t -> p a (n t)")
+
+        def load_w(c):
+            nc.sync.dma_start(out=w_sb[c][:], in_=w_view[:, :, c * 2 * M : (c + 1) * 2 * M].bitcast(I32))
+
+        nc.sync.dma_start(offs_sb[:], offs)
+        nc.sync.dma_start(out=wgt_sb[0][:], in_=wgt[:, 0:SH])
+        nc.sync.dma_start(out=x_sb[0][0][:], in_=x_view[0, 0])
+        nc.sync.dma_start(out=wgt_sb[1][:], in_=wgt[:, SH:S])
+        for a in range(PASSES):
+            for i in range(PACK):
+                if (a, i) != (0, 0):
+                    nc.sync.dma_start(out=x_sb[a][i][:], in_=x_view[a, i])
+        load_w(0)
+        nc.sync.dma_start(offs2_sb[:], offs2)
+        nc.sync.dma_start(out=wgo_sb[0][:], in_=wgo[:, 0:SH])
+        load_w(1)
+        nc.sync.dma_start(out=wgo_sb[1][:], in_=wgo[:, SH:S])
+
+        nc.gpsimd.memset(warm[:], 0.0)
+        nc.scalar.activation(warm[:], warm[:], SILU)
+        nc.gpsimd.memset(ws_sb[:].bitcast(I32), 0)
+        for q in range(4):
+            nc.gpsimd.dma_start(
+                out=ws_sb[32 * q : 32 * q + 8, :].bitcast(I32),
+                in_=w_scales[:, 4 * q : 4 * q + 4, :].bitcast(I32),
+            )
+        nc.gpsimd.memset(brow[:], 0.0)
+        nc.gpsimd.dma_start(out=brow[0:ROW_TILES, :], in_=b.rearrange("(r p) -> r p", p=P))
+        make_identity(nc, ident[:])
+
+        for r in range(ROW_TILES):
+            nc.vector.memset(win_sb[r][:], 0.0)
+
+        bank = psum.tile([P, P], F32, name="bank")
+        nc.tensor.transpose(bank[:], brow[:], ident[:])
+        nc.scalar.copy(bcol[:], bank[:, 0:ROW_TILES])
+
+        def gather(a, i, h):
+            nc.vector.tensor_tensor(
+                g_sb[a][h][:, i, :],
+                x_sb[a][i][:].indirect(offs_sb[:, h * OH : (h + 1) * OH]),
+                wgt_sb[h][:],
+                MULT,
+            )
+
+        def interleave(a, h):
+            nc.scalar.copy(
+                xb_sb[a][h][:].rearrange("p (c e) i -> p c i e", e=4),
+                g_sb[a][h][:].rearrange("p i (c e) -> p c i e", e=4),
+            )
+
+        def quantize(a, h):
+            nc.vector.quantize_mx(
+                out=xq_sb[a][h][:].bitcast(FP8X4),
+                scales=xs_sb[a][h][:],
+                in_=xb_sb[a][h][:].rearrange("p s i -> p (s i)"),
+            )
+
+        def multiply(r, h):
+            acc = psum.tile([P, SH], F32, name="bank")
+            c, col = divmod(r * P, M // 2)
+            for a in range(PASSES):
+                nc.tensor.matmul_mx(
+                    out=acc[:],
+                    lhsT=w_sb[c][:, a, col : col + P].bitcast(FP8X4),
+                    lhsT_scale=ws_sb[4 * a : P, r * P : (r + 1) * P],
+                    rhs=xq_sb[a][h][:].bitcast(FP8X4),
+                    rhs_scale=xs_sb[a][h][:],
+                    start=(a == 0),
+                    stop=(a == PASSES - 1),
+                )
+            y = ypool.tile([P, SH], F32, name="y")
+            nc.scalar.activation(y[:], acc[:], SILU, bias=bcol[:, r : r + 1])
+            return y
+
+        def scatter(r, h, y):
+            nc.vector.tensor_tensor(
+                win_sb[r][:].indirect(offs2_sb[:, h * OH : (h + 1) * OH]), y[:], wgo_sb[h][:], MULT
+            )
+
+        for i in range(PACK):
+            for h in range(HALVES):
+                gather(0, i, h)
+        interleave(0, 0)
+        interleave(0, 1)
+        gather(1, 0, 0)
+        gather(1, 1, 0)
+        quantize(0, 0)
+        gather(1, 0, 1)
+        gather(1, 2, 0)
+        quantize(0, 1)
+        gather(1, 1, 1)
+        gather(1, 3, 0)
+        interleave(1, 0)
+        gather(1, 2, 1)
+        gather(1, 3, 1)
+        quantize(1, 0)
+        ys = [multiply(r, 0) for r in range(2)]
+        interleave(1, 1)
+        ys = ys + [multiply(r, 0) for r in range(2, ROW_TILES)]
+        for r in range(2):
+            scatter(r, 0, ys[r])
+        quantize(1, 1)
+        for r in range(2, ROW_TILES):
+            scatter(r, 0, ys[r])
+        for r in range(ROW_TILES):
+            scatter(r, 1, multiply(r, 1))
+            nc.sync.dma_start(out=out[r * P : (r + 1) * P, :], in_=win_sb[r][:])

@@ -13,6 +13,7 @@ ROW_TILES = M // P
 HALVES = 2
 SH = S // HALVES
 OH = SH // 16
+VECTOR_SHARE = 176
 
 F32 = mybir.dt.float32
 BF16 = mybir.dt.bfloat16
@@ -81,8 +82,11 @@ def tile_list_hboth_silu_kernel(tc, xT, w_words, w_scales, wgt, b, wgo, offs, of
         nc.gpsimd.dma_start(out=brow[0:ROW_TILES, :], in_=b.rearrange("(r p) -> r p", p=P))
         make_identity(nc, ident[:])
 
-        for r in range(ROW_TILES):
-            nc.vector.memset(win_sb[r][:], 0.0)
+        def clear(r):
+            nc.vector.memset(win_sb[r][:].bitcast(I32), 0)
+
+        for r in range(6):
+            clear(r)
 
         bank = psum.tile([P, P], F32, name="bank")
         nc.tensor.transpose(bank[:], brow[:], ident[:])
@@ -101,6 +105,13 @@ def tile_list_hboth_silu_kernel(tc, xT, w_words, w_scales, wgt, b, wgo, offs, of
                 xb_sb[a][h][:].rearrange("p (c e) i -> p c i e", e=4),
                 g_sb[a][h][:].rearrange("p i (c e) -> p c i e", e=4),
             )
+
+        def interleave_shared(a, h):
+            for engine_copy, part in ((nc.vector.tensor_copy, slice(0, VECTOR_SHARE)), (nc.scalar.copy, slice(VECTOR_SHARE, SH))):
+                engine_copy(
+                    xb_sb[a][h][:, part, :].rearrange("p (c e) i -> p c i e", e=4),
+                    g_sb[a][h][:, :, part].rearrange("p i (c e) -> p c i e", e=4),
+                )
 
         def quantize(a, h):
             nc.vector.quantize_mx(
@@ -144,13 +155,15 @@ def tile_list_hboth_silu_kernel(tc, xT, w_words, w_scales, wgt, b, wgo, offs, of
         quantize(0, 1)
         gather(1, 1, 1)
         gather(1, 3, 0)
-        interleave(1, 0)
         gather(1, 2, 1)
+        interleave_shared(1, 0)
         gather(1, 3, 1)
         quantize(1, 0)
         ys = [multiply(r, 0) for r in range(2)]
         interleave(1, 1)
         ys = ys + [multiply(r, 0) for r in range(2, ROW_TILES)]
+        clear(6)
+        clear(7)
         for r in range(2):
             scatter(r, 0, ys[r])
         quantize(1, 1)

@@ -14,6 +14,7 @@ HALVES = 2
 SH = S // HALVES
 OH = SH // 16
 VECTOR_SHARE = 176
+WINDOWS = 4
 
 F32 = mybir.dt.float32
 BF16 = mybir.dt.bfloat16
@@ -44,7 +45,7 @@ def tile_list_hboth_silu_kernel(tc, xT, w_words, w_scales, wgt, b, wgo, offs, of
         xs_sb = [[keep.tile([P, SH], U8, name=f"xs{a}_{h}", align_bytes=64) for h in range(HALVES)] for a in range(PASSES)]
         w_sb = [keep.tile([P, PASSES, M // 2], I32, name=f"w{c}", align_bytes=64) for c in range(2)]
         ws_sb = keep.tile([P, M], U8, name="ws_sb", align_bytes=64)
-        win_sb = [keep.tile([P, T], F32, name=f"win{r}") for r in range(ROW_TILES)]
+        win_sb = [keep.tile([P, T], F32, name=f"win{r}") for r in range(WINDOWS)]
         brow = keep.tile([P, P], F32, name="brow")
         ident = keep.tile([P, P], F32, name="ident")
         bcol = keep.tile([P, ROW_TILES], F32, name="bcol")
@@ -72,21 +73,18 @@ def tile_list_hboth_silu_kernel(tc, xT, w_words, w_scales, wgt, b, wgo, offs, of
 
         nc.gpsimd.memset(warm[:], 0.0)
         nc.scalar.activation(warm[:], warm[:], SILU)
+        make_identity(nc, ident[:])
+        nc.gpsimd.memset(brow[:], 0.0)
         nc.gpsimd.memset(ws_sb[:].bitcast(I32), 0)
         for q in range(4):
             nc.gpsimd.dma_start(
                 out=ws_sb[32 * q : 32 * q + 8, :].bitcast(I32),
                 in_=w_scales[:, 4 * q : 4 * q + 4, :].bitcast(I32),
             )
-        nc.gpsimd.memset(brow[:], 0.0)
         nc.gpsimd.dma_start(out=brow[0:ROW_TILES, :], in_=b.rearrange("(r p) -> r p", p=P))
-        make_identity(nc, ident[:])
 
-        def clear(r):
-            nc.vector.memset(win_sb[r][:].bitcast(I32), 0)
-
-        for r in range(6):
-            clear(r)
+        for w in range(WINDOWS):
+            nc.vector.memset(win_sb[w][:].bitcast(I32), 0)
 
         bank = psum.tile([P, P], F32, name="bank")
         nc.tensor.transpose(bank[:], brow[:], ident[:])
@@ -139,7 +137,7 @@ def tile_list_hboth_silu_kernel(tc, xT, w_words, w_scales, wgt, b, wgo, offs, of
 
         def scatter(r, h, y):
             nc.vector.tensor_tensor(
-                win_sb[r][:].indirect(offs2_sb[:, h * OH : (h + 1) * OH]), y[:], wgo_sb[h][:], MULT
+                win_sb[r % WINDOWS][:].indirect(offs2_sb[:, h * OH : (h + 1) * OH]), y[:], wgo_sb[h][:], MULT
             )
 
         for i in range(PACK):
@@ -150,25 +148,21 @@ def tile_list_hboth_silu_kernel(tc, xT, w_words, w_scales, wgt, b, wgo, offs, of
         gather(1, 0, 0)
         gather(1, 1, 0)
         quantize(0, 0)
-        gather(1, 0, 1)
         gather(1, 2, 0)
-        quantize(0, 1)
-        gather(1, 1, 1)
+        gather(1, 0, 1)
         gather(1, 3, 0)
-        gather(1, 2, 1)
+        gather(1, 1, 1)
         interleave_shared(1, 0)
-        gather(1, 3, 1)
+        quantize(0, 1)
         quantize(1, 0)
-        ys = [multiply(r, 0) for r in range(2)]
-        interleave(1, 1)
-        ys = ys + [multiply(r, 0) for r in range(2, ROW_TILES)]
-        clear(6)
-        clear(7)
-        for r in range(2):
-            scatter(r, 0, ys[r])
-        quantize(1, 1)
-        for r in range(2, ROW_TILES):
-            scatter(r, 0, ys[r])
-        for r in range(ROW_TILES):
-            scatter(r, 1, multiply(r, 1))
-            nc.sync.dma_start(out=out[r * P : (r + 1) * P, :], in_=win_sb[r][:])
+        gather(1, 2, 1)
+        gather(1, 3, 1)
+        for base in range(0, ROW_TILES, WINDOWS):
+            for h in range(HALVES):
+                for r in range(base, base + WINDOWS):
+                    scatter(r, h, multiply(r, h))
+                    if h == HALVES - 1:
+                        nc.sync.dma_start(out=out[r * P : (r + 1) * P, :], in_=win_sb[r % WINDOWS][:])
+                    if (r, h) == (1, 0):
+                        interleave(1, 1)
+                        quantize(1, 1)

from contextlib import ExitStack

import concourse.mybir as mybir
from concourse.masks import make_identity

K, M, T, S = 1024, 1024, 1024, 512
FLOPS = 2 * K * M * S

P = 128
PACK = 4
PASSES = K // (P * PACK)
ROW_TILES = M // P
HALVES = 2
SH = S // HALVES
OH = SH // 16
VECTOR_SHARE = 176
WINDOWS = 4

F32 = mybir.dt.float32
BF16 = mybir.dt.bfloat16
I32 = mybir.dt.int32
U32 = mybir.dt.uint32
U16 = mybir.dt.uint16
U8 = mybir.dt.uint8
FP8X4 = mybir.dt.float8_e4m3fn_x4
MULT = mybir.AluOpType.mult
SILU = mybir.ActivationFunctionType.Silu


def tile_list_hboth_silu_kernel(tc, xT, w_words, w_scales, wgt, b, wgo, offs, offs2, out):
    nc = tc.nc
    with ExitStack() as ctx:
        keep = ctx.enter_context(tc.tile_pool(name="keep", bufs=1))
        ypool = ctx.enter_context(tc.tile_pool(name="ypool", bufs=16))
        psum = ctx.enter_context(tc.psum_pool(name="psum", bufs=8))

        offs_sb = keep.tile([P, S // 16], U16, name="offs_sb")
        offs2_sb = keep.tile([P, S // 16], U16, name="offs2_sb")
        wgt_sb = [keep.tile([P, SH], F32, name=f"wgt{h}") for h in range(HALVES)]
        wgo_sb = [keep.tile([P, SH], F32, name=f"wgo{h}") for h in range(HALVES)]
        x_sb = [[keep.tile([P, T], F32, name=f"x{a}_{i}") for i in range(PACK)] for a in range(PASSES)]
        g_sb = [[keep.tile([P, PACK, SH], F32, name=f"g{a}_{h}") for h in range(HALVES)] for a in range(PASSES)]
        xb_sb = [[keep.tile([P, SH, PACK], BF16, name=f"xb{a}_{h}", align_bytes=64) for h in range(HALVES)] for a in range(PASSES)]
        xq_sb = [[keep.tile([P, SH], U32, name=f"xq{a}_{h}", align_bytes=64) for h in range(HALVES)] for a in range(PASSES)]
        xs_sb = [[keep.tile([P, SH], U8, name=f"xs{a}_{h}", align_bytes=64) for h in range(HALVES)] for a in range(PASSES)]
        w_sb = [keep.tile([P, PASSES, M // 2], I32, name=f"w{c}", align_bytes=64) for c in range(2)]
        ws_sb = keep.tile([P, M], U8, name="ws_sb", align_bytes=64)
        win_sb = [keep.tile([P, T], F32, name=f"win{r}") for r in range(WINDOWS)]
        brow = keep.tile([P, P], F32, name="brow")
        ident = keep.tile([P, P], F32, name="ident")
        bcol = keep.tile([P, ROW_TILES], F32, name="bcol")
        warm = keep.tile([P, 1], F32, name="warm")

        x_view = xT.rearrange("(a p i) t -> a i p t", p=P, i=PACK)
        w_view = w_words.rearrange("a p n t -> p a (n t)")

        def load_w(c):
            nc.sync.dma_start(out=w_sb[c][:], in_=w_view[:, :, c * 2 * M : (c + 1) * 2 * M].bitcast(I32))

        nc.sync.dma_start(offs_sb[:], offs)
        nc.sync.dma_start(out=wgt_sb[0][:], in_=wgt[:, 0:SH])
        nc.sync.dma_start(out=x_sb[0][0][:], in_=x_view[0, 0])
        nc.sync.dma_start(out=wgt_sb[1][:], in_=wgt[:, SH:S])
        for a in range(PASSES):
            for i in range(PACK):
                if (a, i) != (0, 0):
                    nc.sync.dma_start(out=x_sb[a][i][:], in_=x_view[a, i])
        load_w(0)
        nc.sync.dma_start(offs2_sb[:], offs2)
        nc.sync.dma_start(out=wgo_sb[0][:], in_=wgo[:, 0:SH])
        load_w(1)
        nc.sync.dma_start(out=wgo_sb[1][:], in_=wgo[:, SH:S])

        nc.gpsimd.memset(warm[:], 0.0)
        nc.scalar.activation(warm[:], warm[:], SILU)
        make_identity(nc, ident[:])
        nc.gpsimd.memset(brow[:], 0.0)
        nc.gpsimd.memset(ws_sb[:].bitcast(I32), 0)
        for q in range(4):
            nc.gpsimd.dma_start(
                out=ws_sb[32 * q : 32 * q + 8, :].bitcast(I32),
                in_=w_scales[:, 4 * q : 4 * q + 4, :].bitcast(I32),
            )
        nc.gpsimd.dma_start(out=brow[0:ROW_TILES, :], in_=b.rearrange("(r p) -> r p", p=P))

        for w in range(WINDOWS):
            nc.vector.memset(win_sb[w][:].bitcast(I32), 0)

        bank = psum.tile([P, P], F32, name="bank")
        nc.tensor.transpose(bank[:], brow[:], ident[:])
        nc.scalar.copy(bcol[:], bank[:, 0:ROW_TILES])

        def gather(a, i, h):
            nc.vector.tensor_tensor(
                g_sb[a][h][:, i, :],
                x_sb[a][i][:].indirect(offs_sb[:, h * OH : (h + 1) * OH]),
                wgt_sb[h][:],
                MULT,
            )

        def interleave(a, h):
            nc.scalar.copy(
                xb_sb[a][h][:].rearrange("p (c e) i -> p c i e", e=4),
                g_sb[a][h][:].rearrange("p i (c e) -> p c i e", e=4),
            )

        def interleave_shared(a, h):
            for engine_copy, part in ((nc.vector.tensor_copy, slice(0, VECTOR_SHARE)), (nc.scalar.copy, slice(VECTOR_SHARE, SH))):
                engine_copy(
                    xb_sb[a][h][:, part, :].rearrange("p (c e) i -> p c i e", e=4),
                    g_sb[a][h][:, :, part].rearrange("p i (c e) -> p c i e", e=4),
                )

        def quantize(a, h):
            nc.vector.quantize_mx(
                out=xq_sb[a][h][:].bitcast(FP8X4),
                scales=xs_sb[a][h][:],
                in_=xb_sb[a][h][:].rearrange("p s i -> p (s i)"),
            )

        def multiply(r, h):
            acc = psum.tile([P, SH], F32, name="bank")
            c, col = divmod(r * P, M // 2)
            for a in range(PASSES):
                nc.tensor.matmul_mx(
                    out=acc[:],
                    lhsT=w_sb[c][:, a, col : col + P].bitcast(FP8X4),
                    lhsT_scale=ws_sb[4 * a : P, r * P : (r + 1) * P],
                    rhs=xq_sb[a][h][:].bitcast(FP8X4),
                    rhs_scale=xs_sb[a][h][:],
                    start=(a == 0),
                    stop=(a == PASSES - 1),
                )
            y = ypool.tile([P, SH], F32, name="y")
            nc.scalar.activation(y[:], acc[:], SILU, bias=bcol[:, r : r + 1])
            return y

        def scatter(r, h, y):
            nc.vector.tensor_tensor(
                win_sb[r % WINDOWS][:].indirect(offs2_sb[:, h * OH : (h + 1) * OH]), y[:], wgo_sb[h][:], MULT
            )

        for i in range(PACK):
            for h in range(HALVES):
                gather(0, i, h)
        interleave(0, 0)
        interleave(0, 1)
        gather(1, 0, 0)
        gather(1, 1, 0)
        quantize(0, 0)
        gather(1, 2, 0)
        gather(1, 0, 1)
        gather(1, 3, 0)
        gather(1, 1, 1)
        interleave_shared(1, 0)
        quantize(0, 1)
        quantize(1, 0)
        gather(1, 2, 1)
        gather(1, 3, 1)
        for base in range(0, ROW_TILES, WINDOWS):
            for h in range(HALVES):
                for r in range(base, base + WINDOWS):
                    scatter(r, h, multiply(r, h))
                    if h == HALVES - 1:
                        nc.sync.dma_start(out=out[r * P : (r + 1) * P, :], in_=win_sb[r % WINDOWS][:])
                    if (r, h) == (1, 0):
                        interleave(1, 1)
                        quantize(1, 1)
